import numpy as np
import ml_dtypes


def mxq(x, axis, fmt="e4m3"):
    dtype, down = {"e4m3": (ml_dtypes.float8_e4m3fn, 7), "e5m2": (ml_dtypes.float8_e5m2, 14)}[fmt]
    v = np.moveaxis(np.asarray(x, np.float32).astype(ml_dtypes.bfloat16).astype(np.float64), axis, -1)
    blocks = v.reshape(v.shape[:-1] + (-1, 32))
    amax = np.abs(blocks).max(-1, keepdims=True)
    byte = np.maximum(np.where(amax > 0, np.frexp(amax)[1] - 1 + 127, 0) - down, 1)
    scale = np.exp2(byte - 127.0)
    codes = (blocks / scale).astype(np.float32).astype(dtype).astype(np.float64)
    return np.moveaxis((codes * scale).reshape(v.shape), -1, axis)


WIDE = False


def mx_kscale(k):
    if not WIDE:
        return np.ones(k)
    levels = np.array([10, -10, 5, -5, 0])
    if k % 512:
        return np.exp2(np.random.permutation(np.resize(levels, k // 32))).repeat(32)
    a = np.empty((k // 512, 16))
    for p in range(k // 512):
        a[p, :8] = np.random.permutation(np.resize(levels, 8))
        for g in range(8):
            far = levels[np.abs(levels - a[p, g]) >= 10]
            a[p, g + 8] = far[np.random.randint(len(far))]
    return np.exp2(a.ravel()).repeat(32)


def f64(x):
    return np.asarray(x).astype(np.float64)


def striped(idx):
    return np.tile(idx.reshape(-1, 16).T, (8, 1)).astype(np.uint16)


def unstriped(offs):
    return offs[:16].T.reshape(-1).astype(np.int64)


def striped8(idx):
    return np.concatenate([x.reshape(-1, 16).T for x in idx]).astype(np.uint16)


def runs(offs, k):
    lists = np.stack([offs[16 * r : 16 * r + 16].T.reshape(-1) for r in range(8)]).astype(np.int64)
    return lists[np.arange(k) % 512 // 64]


def pack_weight(w):
    k, n = w.shape
    w = f64(np.asarray(w, np.float32).astype(ml_dtypes.bfloat16)).reshape(k // 32, 32, n)
    amax = np.abs(w).max(1)
    byte = np.clip(np.where(amax > 0, np.frexp(amax)[1] - 1 + 127 - 7, 1), 1, 254)
    scaled = (w * np.exp2(127.0 - byte)[:, None, :]).reshape(k, n).astype(np.float32)
    words = np.ascontiguousarray(scaled.reshape(k // 512, 128, 4, n).transpose(0, 1, 3, 2)).astype(ml_dtypes.float8_e4m3fn).view(np.uint8)
    return words, np.ascontiguousarray(byte.astype(np.uint8).reshape(k // 512, 16, n))


def unpack_weight(words, scales):
    g, p, n, _ = words.shape
    vals = np.ascontiguousarray(words).view(ml_dtypes.float8_e4m3fn).astype(np.float64) * np.repeat(np.exp2(scales.astype(np.float64) - 127.0), 8, axis=1)[..., None]
    return vals.transpose(0, 1, 3, 2).reshape(g * 512, n)


E2M1 = np.array([0.0, 0.5, 1.0, 1.5, 2.0, 3.0, 4.0, 6.0, -0.0, -0.5, -1.0, -1.5, -2.0, -3.0, -4.0, -6.0])


def pack_fp4(w):
    k, n = w.shape
    w = f64(np.asarray(w, np.float32).astype(ml_dtypes.bfloat16)).reshape(k // 32, 32, n)
    amax = np.abs(w).max(1)
    mant, ex = np.frexp(amax / 6.0)
    byte = np.clip(np.where(amax > 0, np.where(mant > 0.5, ex, ex - 1) + 127, 1), 1, 254)
    scaled = (w * np.exp2(127.0 - byte)[:, None, :]).reshape(k, n).astype(np.float32)
    c = np.ascontiguousarray(scaled.reshape(k // 512, 128, 4, n).transpose(0, 1, 3, 2)).astype(ml_dtypes.float4_e2m1fn).view(np.uint8) & 0xF
    words = (c[..., 0::2] | (c[..., 1::2] << 4)).reshape(k // 512, 128, 2 * n)
    return np.ascontiguousarray(words), np.ascontiguousarray(byte.astype(np.uint8).reshape(k // 512, 16, n))


def unpack_fp4(words, scales):
    g, _, n = scales.shape
    words = np.ascontiguousarray(words).reshape(g, 128, n, 2)
    nib = np.empty((g, 128, n, 4), np.uint8)
    nib[..., 0::2] = words & 0xF
    nib[..., 1::2] = words >> 4
    vals = E2M1[nib] * np.repeat(np.exp2(scales.astype(np.float64) - 127.0), 8, axis=1)[..., None]
    return vals.transpose(0, 1, 3, 2).reshape(g * 512, n)


def planes(y):
    n, m = y.shape
    v = y.astype(np.float32).astype(ml_dtypes.bfloat16).astype(np.float64).reshape(n // 32, 32, m)
    top = np.abs(v).max(1)
    byte = np.clip(np.where(top > 0, np.frexp(top)[1] - 1 + 127 - 7, 1), 1, 254)
    codes = (v * np.exp2(127.0 - byte)[:, None, :]).reshape(n, m).astype(np.float32).astype(ml_dtypes.float8_e4m3fn).view(np.uint8)
    words = codes.reshape(n // 512, 128, 4, m).transpose(0, 1, 3, 2)
    return np.ascontiguousarray(words), np.ascontiguousarray(byte.astype(np.uint8).reshape(n // 512, 16, m))


K, T, S, H, C = 512, 2048, 256, 512, 512


def setup_inputs():
    n = np.random.standard_normal
    s = mx_kscale(K)[:, None]
    packed_xT = pack_weight(n((K, T)) * s)
    packed_w1 = pack_fp4(n((K, H)) / np.sqrt(K) / s)
    return {
        "x_words": packed_xT[0],
        "x_scales": packed_xT[1],
        "w1_words": packed_w1[0],
        "w1_scales": packed_w1[1],
        "tau": np.random.uniform(0.3, 0.9, (H, 1)).astype(np.float32),
        "gs": (np.random.uniform(0.5, 1.5, (K, 1)) / s).astype(np.float32),
        "tau2": np.random.uniform(0.3, 0.9, (C, 1)).astype(np.float32),
        "offs": striped(np.random.permutation(T)[:S]),
        "n1": striped(np.random.permutation(S)),
        "n2": striped(np.random.permutation(S)),
        "cand": striped(np.random.permutation(T)[:C]),
        "n3": striped8(np.stack([np.random.permutation(S) for _ in range(8)])),
        "n4": striped8(np.stack([np.random.permutation(S) for _ in range(8)])),
    }


def reference(x_words, x_scales, w1_words, w1_scales, tau, gs, tau2, offs, n1, n2, cand, n3, n4):
    x_cand = unpack_weight(x_words, x_scales)[:, unstriped(cand)]
    xq = unpack_weight(x_words, x_scales)[:, unstriped(offs)]
    y = unpack_fp4(w1_words, w1_scales).T @ xq
    sq = (y) ** 2
    ea = np.exp(-1.0 * (f64(tau) * sq[:, unstriped(n1)]))
    z = f64(gs) * (y * ea - (0.5 * y[:, unstriped(n2)]))
    s = 0.0625 * ((x_cand.T @ mxq(z, 0, "e4m3")))
    top = s.max(axis=1, keepdims=True)
    ea2 = np.exp(f64(tau2) * (s[np.arange(C)[:, None], runs(n4, C)] - top))
    out_0 = (0.5 * (s - (s[np.arange(C)[:, None], runs(n3, C)]))) / (ea2 + 0.25)
    return (out_0,) + planes(out_0)

@@ -1,0 +1,210 @@
+from contextlib import ExitStack
+
+import concourse.mybir as mybir
+
+K, T, S, H, C = 512, 2048, 256, 512, 512
+FLOPS = 2 * K * H * S + 2 * K * C * S
+
+F32 = mybir.dt.float32
+BF16 = mybir.dt.bfloat16
+I32 = mybir.dt.int32
+U32 = mybir.dt.uint32
+U16 = mybir.dt.uint16
+U8 = mybir.dt.uint8
+FP8X4 = mybir.dt.float8_e4m3fn_x4
+FP4X4 = mybir.dt.float4_e2m1fn_x4
+ALU = mybir.AluOpType
+ACT = mybir.ActivationFunctionType
+
+P = 128
+PACK = 4
+QUADS = 4
+HALVES = 2
+HALF = S // HALVES
+LIST_COLS = HALF // 16
+
+
+def tile_picked_candegaera_none_po_kernel(
+    tc, x_words, x_scales, w1_words, w1_scales, tau, gs, tau2, offs, n1, n2, cand, n3, n4, out_0, out_1, out_2
+):
+    nc = tc.nc
+    with ExitStack() as ctx:
+        sb = ctx.enter_context(tc.tile_pool(name="sb", bufs=1))
+        ps = ctx.enter_context(tc.psum_pool(name="ps", bufs=1))
+
+        def sbt(name, shape, dtype, tag=""):
+            return sb.tile(shape, dtype, name=name, tag=tag, align_bytes=64)
+
+        def load_list(name, src):
+            lst = sbt(name, list(src.shape), U16)
+            nc.sync.dma_start(lst[:], src)
+            return lst
+
+        def load_rows(name, src):
+            col = sbt(name, [P, PACK], F32)
+            nc.gpsimd.dma_start(col[:], src.rearrange("(p t) o -> p (t o)", t=PACK))
+            return col
+
+        def load_scale_rows(queue, plane, src, quads):
+            for q in quads:
+                rows = src[0, 4 * q : 4 * q + 4, :].bitcast(I32)
+                queue.dma_start(plane[32 * q : 32 * q + 32, :].bitcast(I32), rows.partition_broadcast(8))
+
+        def cols(h):
+            return slice(h * HALF, (h + 1) * HALF)
+
+        def part(lst, h):
+            return lst[:, h * LIST_COLS : (h + 1) * LIST_COLS]
+
+        xs = sbt("xs", [P, T], U8)
+        ws = sbt("ws", [P, H], U8, tag="ws_then_xc")
+
+        load_scale_rows(nc.sync, xs, x_scales, range(QUADS))
+        offs_l = load_list("offs_l", offs)
+        cand_l = load_list("cand_l", cand)
+        xw = sbt("xw", [P, T], U32)
+        nc.sync.dma_start(xw[:].bitcast(I32), x_words[0].rearrange("p n t -> p (n t)").bitcast(I32))
+        ww = sbt("ww", [P, 2 * H], U8)
+        nc.sync.dma_start(ww[:].bitcast(I32), w1_words[0].bitcast(I32))
+        load_scale_rows(nc.sync, ws, w1_scales, range(QUADS))
+        tau_c = load_rows("tau_c", tau)
+        gs_c = load_rows("gs_c", gs)
+        tau2_c = load_rows("tau2_c", tau2)
+        n1_l = load_list("n1_l", n1)
+        n2_l = load_list("n2_l", n2)
+        n3_l = load_list("n3_l", n3)
+        n4_l = load_list("n4_l", n4)
+
+        xq_s = sbt("xq_s", [P, S], U8)
+        nc.vector.tensor_copy(xq_s[:], xs[:].indirect(offs_l[:]))
+        xc_s = sbt("xc_s", [P, C], U8)
+        nc.vector.tensor_copy(xc_s[:].rearrange("p (t m) -> p m t", t=PACK), xs[:].indirect(cand_l[:]))
+        wd_w = sbt("wd_w", [P, 2 * H], U8)
+        nc.scalar.copy(
+            wd_w[:].bitcast(U16).rearrange("p (t m) -> p t m", t=PACK),
+            ww[:].bitcast(U16).rearrange("p (m t) -> p t m", t=PACK),
+        )
+        neg_tau = sbt("neg_tau", [P, PACK], F32)
+        nc.scalar.activation(neg_tau[:], tau_c[:], ACT.Copy, scale=-1.0)
+
+        xq_w = sbt("xq_w", [P, S], U32)
+        nc.vector.tensor_copy(xq_w[:], xw[:].indirect(offs_l[:]))
+        wd_s = sbt("wd_s", [P, H], U8)
+        nc.vector.tensor_copy(
+            wd_s[:].rearrange("p (t m) -> p t m", t=PACK), ws[:].rearrange("p (m t) -> p t m", t=PACK)
+        )
+        xc_w = sbt("xc_w", [P, C], U32, tag="ws_then_xc")
+        nc.vector.tensor_copy(xc_w[:].rearrange("p (t m) -> p m t", t=PACK), xw[:].indirect(cand_l[:]))
+
+        y_ps = []
+        for t in range(PACK):
+            bank = ps.tile([P, S], F32, name=f"y_ps{t}")
+            nc.tensor.matmul_mx(
+                out=bank[:],
+                lhsT=wd_w[:, 2 * P * t : 2 * P * (t + 1)].bitcast(FP4X4),
+                lhsT_scale=wd_s[:, P * t : P * (t + 1)],
+                rhs=xq_w[:].bitcast(FP8X4),
+                rhs_scale=xq_s[:],
+                start=True,
+                stop=True,
+            )
+            y_ps.append(bank)
+
+        sq = [sbt(f"sq{t}", [P, S], F32) for t in range(PACK)]
+        hy = [sbt(f"hy{t}", [P, S], F32) for t in range(PACK)]
+        ea = [sbt(f"ea{h}", [P, PACK, HALF], F32) for h in range(HALVES)]
+        prod = [sbt(f"prod{h}", [P, PACK, HALF], F32) for h in range(HALVES)]
+        z = [sbt(f"z{h}", [P, PACK, HALF], F32) for h in range(HALVES)]
+        zb = [sbt(f"zb{h}", [P, HALF, PACK], BF16) for h in range(HALVES)]
+        zq_w = [sbt(f"zq_w{h}", [P, HALF], U32) for h in range(HALVES)]
+        zq_s = [sbt(f"zq_s{h}", [P, HALF], U8) for h in range(HALVES)]
+        s_ps = [ps.tile([P, S], F32, name=f"s_ps{t}") for t in range(PACK)]
+
+        for t in range(PACK):
+            nc.scalar.activation(sq[t][:], y_ps[t][:], ACT.Square)
+            if t == 1:
+                nc.vector.tensor_scalar(hy[t][:], y_ps[t][:], gs_c[:, t : t + 1], None, ALU.mult)
+            else:
+                nc.scalar.activation(hy[t][:], y_ps[t][:], ACT.Copy, scale=gs_c[:, t : t + 1])
+            for h in range(HALVES):
+                nc.scalar.activation(
+                    ea[h][:, t, :], sq[t][:].indirect(part(n1_l, h)), ACT.Exp, scale=neg_tau[:, t : t + 1]
+                )
+            for h in range(HALVES):
+                nc.vector.scalar_tensor_tensor(
+                    prod[h][:, t, :], hy[t][:, cols(h)], -2.0, ea[h][:, t, :], ALU.mult, ALU.mult
+                )
+            for h in range(HALVES):
+                nc.vector.tensor_tensor(z[h][:, t, :], hy[t][:].indirect(part(n2_l, h)), prod[h][:, t, :], ALU.add)
+
+        nc.scalar.activation(zb[0][:], z[0][:].rearrange("p t j -> p j t"), ACT.Copy, scale=-0.5)
+        nc.vector.tensor_scalar(zb[1][:], z[1][:].rearrange("p t j -> p j t"), -0.5, None, ALU.mult)
+        for h in range(HALVES):
+            nc.vector.quantize_mx(
+                out=zq_w[h][:].bitcast(FP8X4), scales=zq_s[h][:], in_=zb[h][:].rearrange("p j t -> p (j t)")
+            )
+            for t in range(PACK):
+                nc.tensor.matmul_mx(
+                    out=s_ps[t][:, cols(h)],
+                    lhsT=xc_w[:, P * t : P * (t + 1)].bitcast(FP8X4),
+                    lhsT_scale=xc_s[:, P * t : P * (t + 1)],
+                    rhs=zq_w[h][:].bitcast(FP8X4),
+                    rhs_scale=zq_s[h][:],
+                    start=True,
+                    stop=True,
+                )
+
+        s = [sbt(f"s{t}", [P, S], F32) for t in range(PACK)]
+        top = [sbt(f"top{t}", [P, 1], F32) for t in range(PACK)]
+        bias = [sbt(f"bias{t}", [P, 1], F32) for t in range(PACK)]
+        ea2 = [sbt(f"ea2_{t}", [P, S], F32) for t in range(PACK)]
+        den2 = sbt("den2", [P, PACK, S], F32)
+        s3 = [sbt(f"s3_{h}", [P, PACK, HALF], F32) for h in range(HALVES)]
+        num = [sbt(f"num{h}", [P, PACK, HALF], F32) for h in range(HALVES)]
+        inv = [sbt(f"inv{h}", [P, PACK, HALF], F32) for h in range(HALVES)]
+        res = [sbt(f"res{h}", [P, PACK, HALF], F32) for h in range(HALVES)]
+        rb = [sbt(f"rb{h}", [P, HALF, PACK], BF16) for h in range(HALVES)]
+        rq_w = sbt("rq_w", [P, S], U32)
+        rq_s = sbt("rq_s", [P, S], U8)
+
+        for t in range(PACK):
+            nc.vector.tensor_scalar(s[t][:], s_ps[t][:], 0.0625, None, ALU.mult, ALU.max, accum_out=top[t][:])
+            nc.vector.tensor_scalar(bias[t][:], top[t][:], tau2_c[:, t : t + 1], -1.0, ALU.mult, ALU.mult)
+            nc.scalar.activation(s3[0][:, t, :], s[t][:].indirect(part(n3_l, 0)), ACT.Copy)
+            for h in range(HALVES):
+                nc.scalar.activation(
+                    ea2[t][:, cols(h)],
+                    s[t][:].indirect(part(n4_l, h)),
+                    ACT.Exp,
+                    bias=bias[t][:],
+                    scale=tau2_c[:, t : t + 1],
+                )
+        for t in range(PACK):
+            nc.vector.tensor_tensor(num[0][:, t, :], s[t][:, cols(0)], s3[0][:, t, :], ALU.subtract)
+            nc.vector.scalar_tensor_tensor(den2[:, t, :], ea2[t][:], 0.5, ea2[t][:], ALU.add, ALU.mult)
+
+        out_rows = out_0.rearrange("(p t) j -> p t j", t=PACK)
+        out_words = out_1[0].rearrange("p j r -> p (j r)").bitcast(I32)
+
+        def finish(h, queue):
+            queue.dma_start(out_rows[:, :, cols(h)], res[h][:])
+            nc.vector.tensor_copy(rb[h][:], res[h][:].rearrange("p t j -> p j t"))
+            nc.vector.quantize_mx(
+                out=rq_w[:, cols(h)].bitcast(FP8X4), scales=rq_s[:, cols(h)], in_=rb[h][:].rearrange("p j t -> p (j t)")
+            )
+            queue.dma_start(out_words[:, cols(h)], rq_w[:, cols(h)].bitcast(I32))
+
+        for t in range(0, PACK, 2):
+            pair = slice(t, t + 2)
+            nc.scalar.activation(inv[0][:, pair, :], den2[:, pair, cols(0)], ACT.Abs_reciprocal_sqrt, bias=0.25, scale=4.0)
+            nc.vector.tensor_tensor(res[0][:, pair, :], num[0][:, pair, :], inv[0][:, pair, :], ALU.mult)
+        finish(0, nc.sync)
+        for t in range(PACK):
+            nc.scalar.activation(s3[1][:, t, :], s[t][:].indirect(part(n3_l, 1)), ACT.Copy)
+            nc.vector.tensor_tensor(num[1][:, t, :], s[t][:, cols(1)], s3[1][:, t, :], ALU.subtract)
+        for t in range(PACK):
+            nc.scalar.activation(inv[1][:, t, :], den2[:, t, cols(1)], ACT.Abs_reciprocal_sqrt, bias=0.25, scale=4.0)
+            nc.vector.tensor_tensor(res[1][:, t, :], num[1][:, t, :], inv[1][:, t, :], ALU.mult)
+        finish(1, nc.sync)
+        for q in range(QUADS):
+            nc.scalar.dma_start(out_2[0, 4 * q : 4 * q + 4, :].bitcast(I32), rq_s[32 * q : 32 * q + 4, :].bitcast(I32))

@@ -45,10 +45,12 @@ def tile_picked_candegaera_none_po_kernel(
             nc.gpsimd.dma_start(col[:], src.rearrange("(p t) o -> p (t o)", t=PACK))
             return col
 
-        def load_scale_rows(queue, plane, src, quads):
-            for q in quads:
-                rows = src[0, 4 * q : 4 * q + 4, :].bitcast(I32)
-                queue.dma_start(plane[32 * q : 32 * q + 32, :].bitcast(I32), rows.partition_broadcast(8))
+        def live(plane, q):
+            return plane[32 * q : 32 * q + 4, :].bitcast(I32)
+
+        def load_scale_rows(plane, src):
+            for q in range(QUADS):
+                nc.sync.dma_start(live(plane, q), src[0, 4 * q : 4 * q + 4, :].bitcast(I32))
 
         def cols(h):
             return slice(h * HALF, (h + 1) * HALF)
@@ -59,14 +61,17 @@ def tile_picked_candegaera_none_po_kernel(
         xs = sbt("xs", [P, T], U8)
         ws = sbt("ws", [P, H], U8, tag="ws_then_xc")
 
-        load_scale_rows(nc.sync, xs, x_scales, range(QUADS))
+        nc.vector.memset(xs[:].bitcast(I32), 0)
+        nc.vector.memset(ws[:].bitcast(I32), 0)
+        xs_in = sbt("xs_in", [P, T], U8)
+        load_scale_rows(xs_in, x_scales)
         offs_l = load_list("offs_l", offs)
         cand_l = load_list("cand_l", cand)
         xw = sbt("xw", [P, T], U32)
         nc.sync.dma_start(xw[:].bitcast(I32), x_words[0].rearrange("p n t -> p (n t)").bitcast(I32))
         ww = sbt("ww", [P, 2 * H], U8)
         nc.sync.dma_start(ww[:].bitcast(I32), w1_words[0].bitcast(I32))
-        load_scale_rows(nc.sync, ws, w1_scales, range(QUADS))
+        load_scale_rows(ws, w1_scales)
         tau_c = load_rows("tau_c", tau)
         gs_c = load_rows("gs_c", gs)
         tau2_c = load_rows("tau2_c", tau2)
@@ -75,6 +80,8 @@ def tile_picked_candegaera_none_po_kernel(
         n3_l = load_list("n3_l", n3)
         n4_l = load_list("n4_l", n4)
 
+        for q in range(QUADS):
+            nc.vector.tensor_copy(live(xs, q), live(xs_in, q))
         xq_s = sbt("xq_s", [P, S], U8)
         nc.vector.tensor_copy(xq_s[:], xs[:].indirect(offs_l[:]))
         xc_s = sbt("xc_s", [P, C], U8)
@@ -120,25 +127,50 @@ def tile_picked_candegaera_none_po_kernel(
         zq_s = [sbt(f"zq_s{h}", [P, HALF], U8) for h in range(HALVES)]
         s_ps = [ps.tile([P, S], F32, name=f"s_ps{t}") for t in range(PACK)]
 
-        for t in range(PACK):
+        def square(t):
             nc.scalar.activation(sq[t][:], y_ps[t][:], ACT.Square)
-            if t == 1:
+
+        def weigh(t):
+            if t > 0:
                 nc.vector.tensor_scalar(hy[t][:], y_ps[t][:], gs_c[:, t : t + 1], None, ALU.mult)
             else:
                 nc.scalar.activation(hy[t][:], y_ps[t][:], ACT.Copy, scale=gs_c[:, t : t + 1])
-            for h in range(HALVES):
-                nc.scalar.activation(
-                    ea[h][:, t, :], sq[t][:].indirect(part(n1_l, h)), ACT.Exp, scale=neg_tau[:, t : t + 1]
-                )
-            for h in range(HALVES):
-                nc.vector.scalar_tensor_tensor(
-                    prod[h][:, t, :], hy[t][:, cols(h)], -2.0, ea[h][:, t, :], ALU.mult, ALU.mult
-                )
-            for h in range(HALVES):
-                nc.vector.tensor_tensor(z[h][:, t, :], hy[t][:].indirect(part(n2_l, h)), prod[h][:, t, :], ALU.add)
 
-        nc.scalar.activation(zb[0][:], z[0][:].rearrange("p t j -> p j t"), ACT.Copy, scale=-0.5)
-        nc.vector.tensor_scalar(zb[1][:], z[1][:].rearrange("p t j -> p j t"), -0.5, None, ALU.mult)
+        def damp(t, h):
+            nc.scalar.activation(ea[h][:, t, :], sq[t][:].indirect(part(n1_l, h)), ACT.Exp, scale=neg_tau[:, t : t + 1])
+            nc.vector.scalar_tensor_tensor(prod[h][:, t, :], hy[t][:, cols(h)], -2.0, ea[h][:, t, :], ALU.mult, ALU.mult)
+
+        def pull(t, h):
+            nc.vector.tensor_tensor(z[h][:, t, :], hy[t][:].indirect(part(n2_l, h)), prod[h][:, t, :], ALU.add)
+
+        def woven(planes):
+            return planes.rearrange("p t (c i) -> p c t i", i=4)
+
+        def packed(words):
+            return words.rearrange("p (c i) t -> p c t i", i=4)
+
+        for t in range(2):
+            square(t)
+            weigh(t)
+            damp(t, 0)
+            damp(t, 1)
+            pull(t, 0)
+            pull(t, 1)
+        square(2)
+        weigh(2)
+        damp(2, 0)
+        square(3)
+        weigh(3)
+        pull(2, 0)
+        damp(3, 0)
+        damp(2, 1)
+        pull(3, 0)
+        damp(3, 1)
+        pull(2, 1)
+        pull(3, 1)
+
+        for h in range(HALVES):
+            nc.scalar.activation(packed(zb[h][:]), woven(z[h][:]), ACT.Copy, scale=-0.5)
         for h in range(HALVES):
             nc.vector.quantize_mx(
                 out=zq_w[h][:].bitcast(FP8X4), scales=zq_s[h][:], in_=zb[h][:].rearrange("p j t -> p (j t)")
@@ -188,7 +220,7 @@ def tile_picked_candegaera_none_po_kernel(
 
         def finish(h, queue):
             queue.dma_start(out_rows[:, :, cols(h)], res[h][:])
-            nc.vector.tensor_copy(rb[h][:], res[h][:].rearrange("p t j -> p j t"))
+            nc.vector.tensor_copy(packed(rb[h][:]), woven(res[h][:]))
             nc.vector.quantize_mx(
                 out=rq_w[:, cols(h)].bitcast(FP8X4), scales=rq_s[:, cols(h)], in_=rb[h][:].rearrange("p j t -> p (j t)")
             )
@@ -207,4 +239,5 @@ def tile_picked_candegaera_none_po_kernel(
             nc.vector.tensor_tensor(res[1][:, t, :], num[1][:, t, :], inv[1][:, t, :], ALU.mult)
         finish(1, nc.sync)
         for q in range(QUADS):
-            nc.scalar.dma_start(out_2[0, 4 * q : 4 * q + 4, :].bitcast(I32), rq_s[32 * q : 32 * q + 4, :].bitcast(I32))
+            queue = nc.sync if q == QUADS - 1 else nc.scalar
+            queue.dma_start(out_2[0, 4 * q : 4 * q + 4, :].bitcast(I32), rq_s[32 * q : 32 * q + 4, :].bitcast(I32))

@@ -103,6 +103,7 @@ def tile_picked_candegaera_none_po_kernel(
         xc_w = sbt("xc_w", [P, C], U32, tag="ws_then_xc")
         nc.vector.tensor_copy(xc_w[:].rearrange("p (t m) -> p m t", t=PACK), xw[:].indirect(cand_l[:]))
 
+
         y_ps = []
         for t in range(PACK):
             bank = ps.tile([P, S], F32, name=f"y_ps{t}")
@@ -117,31 +118,17 @@ def tile_picked_candegaera_none_po_kernel(
             )
             y_ps.append(bank)
 
-        sq = [sbt(f"sq{t}", [P, S], F32) for t in range(PACK)]
-        hy = [sbt(f"hy{t}", [P, S], F32) for t in range(PACK)]
-        ea = [sbt(f"ea{h}", [P, PACK, HALF], F32) for h in range(HALVES)]
-        prod = [sbt(f"prod{h}", [P, PACK, HALF], F32) for h in range(HALVES)]
-        z = [sbt(f"z{h}", [P, PACK, HALF], F32) for h in range(HALVES)]
+        sq = [sbt(f"sq{t}", [P, 2 * S], F32) for t in range(PACK)]
+        hy = [sbt(f"hy{t}", [P, 2 * S], F32) for t in range(PACK)]
+        s = [sbt(f"s{t}", [P, 2 * S], F32) for t in range(PACK)]
+        z = sbt("z", [P, PACK, S], F32)
+        pulled = sbt("pulled", [P, S], F32)
         zb = [sbt(f"zb{h}", [P, HALF, PACK], BF16) for h in range(HALVES)]
         zq_w = [sbt(f"zq_w{h}", [P, HALF], U32) for h in range(HALVES)]
         zq_s = [sbt(f"zq_s{h}", [P, HALF], U8) for h in range(HALVES)]
         s_ps = [ps.tile([P, S], F32, name=f"s_ps{t}") for t in range(PACK)]
-
-        def square(t):
-            nc.scalar.activation(sq[t][:], y_ps[t][:], ACT.Square)
-
-        def weigh(t):
-            if t > 0:
-                nc.vector.tensor_scalar(hy[t][:], y_ps[t][:], gs_c[:, t : t + 1], None, ALU.mult)
-            else:
-                nc.scalar.activation(hy[t][:], y_ps[t][:], ACT.Copy, scale=gs_c[:, t : t + 1])
-
-        def damp(t, h):
-            nc.scalar.activation(ea[h][:, t, :], sq[t][:].indirect(part(n1_l, h)), ACT.Exp, scale=neg_tau[:, t : t + 1])
-            nc.vector.scalar_tensor_tensor(prod[h][:, t, :], hy[t][:, cols(h)], -2.0, ea[h][:, t, :], ALU.mult, ALU.mult)
-
-        def pull(t, h):
-            nc.vector.tensor_tensor(z[h][:, t, :], hy[t][:].indirect(part(n2_l, h)), prod[h][:, t, :], ALU.add)
+        for t in range(PACK):
+            nc.vector.memset(sq[t][:, S:], 0.0)
 
         def woven(planes):
             return planes.rearrange("p t (c i) -> p c t i", i=4)
@@ -149,28 +136,32 @@ def tile_picked_candegaera_none_po_kernel(
         def packed(words):
             return words.rearrange("p (c i) t -> p c t i", i=4)
 
-        for t in range(2):
-            square(t)
-            weigh(t)
-            damp(t, 0)
-            damp(t, 1)
-            pull(t, 0)
-            pull(t, 1)
-        square(2)
-        weigh(2)
-        damp(2, 0)
-        square(3)
-        weigh(3)
-        pull(2, 0)
-        damp(3, 0)
-        damp(2, 1)
-        pull(3, 0)
-        damp(3, 1)
-        pull(2, 1)
-        pull(3, 1)
+        def entries(lst, j):
+            return lst[:, j.start // 16 : j.stop // 16]
 
-        for h in range(HALVES):
-            nc.scalar.activation(packed(zb[h][:]), woven(z[h][:]), ACT.Copy, scale=-0.5)
+        for t in range(PACK):
+            ea = hy[t][:, S:]
+            prod = s[t][:, S:]
+            if t == 0:
+                nc.scalar.activation(sq[t][:, :S], y_ps[t][:], ACT.Square)
+                nc.scalar.activation(hy[t][:, :S], y_ps[t][:], ACT.Copy, scale=gs_c[:, t : t + 1])
+            else:
+                nc.vector.tensor_scalar(hy[t][:, :S], y_ps[t][:], gs_c[:, t : t + 1], None, ALU.mult)
+                nc.scalar.activation(sq[t][:, :S], y_ps[t][:], ACT.Square)
+            pieces = [cols(0), cols(1)] if t == PACK - 1 else [slice(0, S)]
+            for j in pieces:
+                nc.scalar.activation(ea[:, j], sq[t][:].indirect(entries(n1_l, j)), ACT.Exp, scale=neg_tau[:, t : t + 1])
+            for j in pieces:
+                nc.vector.scalar_tensor_tensor(prod[:, j], hy[t][:, j], -2.0, ea[:, j], ALU.mult, ALU.mult)
+            for j in pieces:
+                if t == PACK - 1:
+                    nc.scalar.activation(pulled[:, j], hy[t][:].indirect(entries(n2_l, j)), ACT.Copy)
+                    nc.vector.tensor_tensor(z[:, t, j], pulled[:, j], prod[:, j], ALU.add)
+                else:
+                    nc.vector.tensor_tensor(z[:, t, j], hy[t][:].indirect(entries(n2_l, j)), prod[:, j], ALU.add)
+
+        nc.vector.tensor_scalar(packed(zb[0][:]), woven(z[:, :, cols(0)]), -0.5, None, ALU.mult)
+        nc.scalar.activation(packed(zb[1][:]), woven(z[:, :, cols(1)]), ACT.Copy, scale=-0.5)
         for h in range(HALVES):
             nc.vector.quantize_mx(
                 out=zq_w[h][:].bitcast(FP8X4), scales=zq_s[h][:], in_=zb[h][:].rearrange("p j t -> p (j t)")
@@ -186,7 +177,6 @@ def tile_picked_candegaera_none_po_kernel(
                     stop=True,
                 )
 
-        s = [sbt(f"s{t}", [P, S], F32) for t in range(PACK)]
         top = [sbt(f"top{t}", [P, 1], F32) for t in range(PACK)]
         bias = [sbt(f"bias{t}", [P, 1], F32) for t in range(PACK)]
         ea2 = [sbt(f"ea2_{t}", [P, S], F32) for t in range(PACK)]
@@ -200,17 +190,12 @@ def tile_picked_candegaera_none_po_kernel(
         rq_s = sbt("rq_s", [P, S], U8)
 
         for t in range(PACK):
-            nc.vector.tensor_scalar(s[t][:], s_ps[t][:], 0.0625, None, ALU.mult, ALU.max, accum_out=top[t][:])
+            nc.vector.tensor_scalar(s[t][:, :S], s_ps[t][:], 0.0625, None, ALU.mult, ALU.max, accum_out=top[t][:])
             nc.vector.tensor_scalar(bias[t][:], top[t][:], tau2_c[:, t : t + 1], -1.0, ALU.mult, ALU.mult)
             nc.scalar.activation(s3[0][:, t, :], s[t][:].indirect(part(n3_l, 0)), ACT.Copy)
-            for h in range(HALVES):
-                nc.scalar.activation(
-                    ea2[t][:, cols(h)],
-                    s[t][:].indirect(part(n4_l, h)),
-                    ACT.Exp,
-                    bias=bias[t][:],
-                    scale=tau2_c[:, t : t + 1],
-                )
+            nc.scalar.activation(
+                ea2[t][:], s[t][:].indirect(n4_l[:]), ACT.Exp, bias=bias[t][:], scale=tau2_c[:, t : t + 1]
+            )
         for t in range(PACK):
             nc.vector.tensor_tensor(num[0][:, t, :], s[t][:, cols(0)], s3[0][:, t, :], ALU.subtract)
             nc.vector.scalar_tensor_tensor(den2[:, t, :], ea2[t][:], 0.5, ea2[t][:], ALU.add, ALU.mult)

@@ -61,10 +61,14 @@ def tile_picked_candegaera_none_po_kernel(
         xs = sbt("xs", [P, T], U8)
         ws = sbt("ws", [P, H], U8, tag="ws_then_xc")
 
-        nc.vector.memset(xs[:].bitcast(I32), 0)
+        nc.vector.memset(xs[P // 2 :, :].bitcast(I32), 0)
         nc.vector.memset(ws[:].bitcast(I32), 0)
         xs_in = sbt("xs_in", [P, T], U8)
-        load_scale_rows(xs_in, x_scales)
+        for q in (2, 3):
+            nc.sync.dma_start(live(xs_in, q), x_scales[0, 4 * q : 4 * q + 4, :].bitcast(I32))
+        for q in (0, 1):
+            rows = x_scales[0, 4 * q : 4 * q + 4, :].bitcast(I32)
+            nc.sync.dma_start(xs[32 * q : 32 * q + 32, :].bitcast(I32), rows.partition_broadcast(8))
         offs_l = load_list("offs_l", offs)
         cand_l = load_list("cand_l", cand)
         xw = sbt("xw", [P, T], U32)
@@ -80,7 +84,7 @@ def tile_picked_candegaera_none_po_kernel(
         n3_l = load_list("n3_l", n3)
         n4_l = load_list("n4_l", n4)
 
-        for q in range(QUADS):
+        for q in (2, 3):
             nc.vector.tensor_copy(live(xs, q), live(xs_in, q))
         xq_s = sbt("xq_s", [P, S], U8)
         nc.vector.tensor_copy(xq_s[:], xs[:].indirect(offs_l[:]))
@@ -198,7 +202,14 @@ def tile_picked_candegaera_none_po_kernel(
             )
         for t in range(PACK):
             nc.vector.tensor_tensor(num[0][:, t, :], s[t][:, cols(0)], s3[0][:, t, :], ALU.subtract)
-            nc.vector.scalar_tensor_tensor(den2[:, t, :], ea2[t][:], 0.5, ea2[t][:], ALU.add, ALU.mult)
+            if t == PACK - 1:
+                late = ea2[t][:, cols(1)]
+                nc.vector.tensor_scalar(den2[:, t, cols(0)], ea2[t][:, cols(0)], 2.0, 0.5, ALU.mult, ALU.add)
+                nc.vector.scalar_tensor_tensor(den2[:, t, cols(1)], late, 0.5, late, ALU.add, ALU.mult)
+                nc.vector.reciprocal(inv[0][:, t, :], den2[:, t, cols(0)])
+                nc.vector.tensor_tensor(res[0][:, t, :], num[0][:, t, :], inv[0][:, t, :], ALU.mult)
+            else:
+                nc.vector.scalar_tensor_tensor(den2[:, t, :], ea2[t][:], 0.5, ea2[t][:], ALU.add, ALU.mult)
 
         out_rows = out_0.rearrange("(p t) j -> p t j", t=PACK)
         out_words = out_1[0].rearrange("p j r -> p (j r)").bitcast(I32)
@@ -211,8 +222,7 @@ def tile_picked_candegaera_none_po_kernel(
             )
             queue.dma_start(out_words[:, cols(h)], rq_w[:, cols(h)].bitcast(I32))
 
-        for t in range(0, PACK, 2):
-            pair = slice(t, t + 2)
+        for pair in (slice(0, 2), slice(2, 3)):
             nc.scalar.activation(inv[0][:, pair, :], den2[:, pair, cols(0)], ACT.Abs_reciprocal_sqrt, bias=0.25, scale=4.0)
             nc.vector.tensor_tensor(res[0][:, pair, :], num[0][:, pair, :], inv[0][:, pair, :], ALU.mult)
         finish(0, nc.sync)

from contextlib import ExitStack

import concourse.mybir as mybir

K, T, S, H, C = 512, 2048, 256, 512, 512
FLOPS = 2 * K * H * S + 2 * K * C * S

F32 = mybir.dt.float32
BF16 = mybir.dt.bfloat16
I32 = mybir.dt.int32
U32 = mybir.dt.uint32
U16 = mybir.dt.uint16
U8 = mybir.dt.uint8
FP8X4 = mybir.dt.float8_e4m3fn_x4
FP4X4 = mybir.dt.float4_e2m1fn_x4
ALU = mybir.AluOpType
ACT = mybir.ActivationFunctionType

P = 128
PACK = 4
QUADS = 4
HALVES = 2
HALF = S // HALVES
LIST_COLS = HALF // 16


def tile_picked_candegaera_none_po_kernel(
    tc, x_words, x_scales, w1_words, w1_scales, tau, gs, tau2, offs, n1, n2, cand, n3, n4, out_0, out_1, out_2
):
    nc = tc.nc
    with ExitStack() as ctx:
        sb = ctx.enter_context(tc.tile_pool(name="sb", bufs=1))
        ps = ctx.enter_context(tc.psum_pool(name="ps", bufs=1))

        def sbt(name, shape, dtype, tag=""):
            return sb.tile(shape, dtype, name=name, tag=tag, align_bytes=64)

        def load_list(name, src):
            lst = sbt(name, list(src.shape), U16)
            nc.sync.dma_start(lst[:], src)
            return lst

        def load_rows(name, src):
            col = sbt(name, [P, PACK], F32)
            nc.gpsimd.dma_start(col[:], src.rearrange("(p t) o -> p (t o)", t=PACK))
            return col

        def live(plane, q):
            return plane[32 * q : 32 * q + 4, :].bitcast(I32)

        def load_scale_rows(plane, src):
            for q in range(QUADS):
                nc.sync.dma_start(live(plane, q), src[0, 4 * q : 4 * q + 4, :].bitcast(I32))

        def cols(h):
            return slice(h * HALF, (h + 1) * HALF)

        def part(lst, h):
            return lst[:, h * LIST_COLS : (h + 1) * LIST_COLS]

        xs = sbt("xs", [P, T], U8)
        ws = sbt("ws", [P, H], U8, tag="ws_then_xc")

        nc.vector.memset(xs[P // 2 :, :].bitcast(I32), 0)
        nc.vector.memset(ws[:].bitcast(I32), 0)
        xs_in = sbt("xs_in", [P, T], U8)
        for q in (2, 3):
            nc.sync.dma_start(live(xs_in, q), x_scales[0, 4 * q : 4 * q + 4, :].bitcast(I32))
        for q in (0, 1):
            rows = x_scales[0, 4 * q : 4 * q + 4, :].bitcast(I32)
            nc.sync.dma_start(xs[32 * q : 32 * q + 32, :].bitcast(I32), rows.partition_broadcast(8))
        offs_l = load_list("offs_l", offs)
        cand_l = load_list("cand_l", cand)
        xw = sbt("xw", [P, T], U32)
        nc.sync.dma_start(xw[:].bitcast(I32), x_words[0].rearrange("p n t -> p (n t)").bitcast(I32))
        ww = sbt("ww", [P, 2 * H], U8)
        nc.sync.dma_start(ww[:].bitcast(I32), w1_words[0].bitcast(I32))
        load_scale_rows(ws, w1_scales)
        tau_c = load_rows("tau_c", tau)
        gs_c = load_rows("gs_c", gs)
        tau2_c = load_rows("tau2_c", tau2)
        n1_l = load_list("n1_l", n1)
        n2_l = load_list("n2_l", n2)
        n3_l = load_list("n3_l", n3)
        n4_l = load_list("n4_l", n4)

        for q in (2, 3):
            nc.vector.tensor_copy(live(xs, q), live(xs_in, q))
        xq_s = sbt("xq_s", [P, S], U8)
        nc.vector.tensor_copy(xq_s[:], xs[:].indirect(offs_l[:]))
        xc_s = sbt("xc_s", [P, C], U8)
        nc.vector.tensor_copy(xc_s[:].rearrange("p (t m) -> p m t", t=PACK), xs[:].indirect(cand_l[:]))
        wd_w = sbt("wd_w", [P, 2 * H], U8)
        nc.scalar.copy(
            wd_w[:].bitcast(U16).rearrange("p (t m) -> p t m", t=PACK),
            ww[:].bitcast(U16).rearrange("p (m t) -> p t m", t=PACK),
        )
        neg_tau = sbt("neg_tau", [P, PACK], F32)
        nc.scalar.activation(neg_tau[:], tau_c[:], ACT.Copy, scale=-1.0)

        xq_w = sbt("xq_w", [P, S], U32)
        nc.vector.tensor_copy(xq_w[:], xw[:].indirect(offs_l[:]))
        wd_s = sbt("wd_s", [P, H], U8)
        nc.vector.tensor_copy(
            wd_s[:].rearrange("p (t m) -> p t m", t=PACK), ws[:].rearrange("p (m t) -> p t m", t=PACK)
        )
        xc_w = sbt("xc_w", [P, C], U32, tag="ws_then_xc")
        nc.vector.tensor_copy(xc_w[:].rearrange("p (t m) -> p m t", t=PACK), xw[:].indirect(cand_l[:]))


        y_ps = []
        for t in range(PACK):
            bank = ps.tile([P, S], F32, name=f"y_ps{t}")
            nc.tensor.matmul_mx(
                out=bank[:],
                lhsT=wd_w[:, 2 * P * t : 2 * P * (t + 1)].bitcast(FP4X4),
                lhsT_scale=wd_s[:, P * t : P * (t + 1)],
                rhs=xq_w[:].bitcast(FP8X4),
                rhs_scale=xq_s[:],
                start=True,
                stop=True,
            )
            y_ps.append(bank)

        sq = [sbt(f"sq{t}", [P, 2 * S], F32) for t in range(PACK)]
        hy = [sbt(f"hy{t}", [P, 2 * S], F32) for t in range(PACK)]
        s = [sbt(f"s{t}", [P, 2 * S], F32) for t in range(PACK)]
        z = sbt("z", [P, PACK, S], F32)
        pulled = sbt("pulled", [P, S], F32)
        zb = [sbt(f"zb{h}", [P, HALF, PACK], BF16) for h in range(HALVES)]
        zq_w = [sbt(f"zq_w{h}", [P, HALF], U32) for h in range(HALVES)]
        zq_s = [sbt(f"zq_s{h}", [P, HALF], U8) for h in range(HALVES)]
        s_ps = [ps.tile([P, S], F32, name=f"s_ps{t}") for t in range(PACK)]
        for t in range(PACK):
            nc.vector.memset(sq[t][:, S:], 0.0)

        def woven(planes):
            return planes.rearrange("p t (c i) -> p c t i", i=4)

        def packed(words):
            return words.rearrange("p (c i) t -> p c t i", i=4)

        def entries(lst, j):
            return lst[:, j.start // 16 : j.stop // 16]

        for t in range(PACK):
            ea = hy[t][:, S:]
            prod = s[t][:, S:]
            if t == 0:
                nc.scalar.activation(sq[t][:, :S], y_ps[t][:], ACT.Square)
                nc.scalar.activation(hy[t][:, :S], y_ps[t][:], ACT.Copy, scale=gs_c[:, t : t + 1])
            else:
                nc.vector.tensor_scalar(hy[t][:, :S], y_ps[t][:], gs_c[:, t : t + 1], None, ALU.mult)
                nc.scalar.activation(sq[t][:, :S], y_ps[t][:], ACT.Square)
            pieces = [cols(0), cols(1)] if t == PACK - 1 else [slice(0, S)]
            for j in pieces:
                nc.scalar.activation(ea[:, j], sq[t][:].indirect(entries(n1_l, j)), ACT.Exp, scale=neg_tau[:, t : t + 1])
            for j in pieces:
                nc.vector.scalar_tensor_tensor(prod[:, j], hy[t][:, j], -2.0, ea[:, j], ALU.mult, ALU.mult)
            for j in pieces:
                if t == PACK - 1:
                    nc.scalar.activation(pulled[:, j], hy[t][:].indirect(entries(n2_l, j)), ACT.Copy)
                    nc.vector.tensor_tensor(z[:, t, j], pulled[:, j], prod[:, j], ALU.add)
                else:
                    nc.vector.tensor_tensor(z[:, t, j], hy[t][:].indirect(entries(n2_l, j)), prod[:, j], ALU.add)

        nc.vector.tensor_scalar(packed(zb[0][:]), woven(z[:, :, cols(0)]), -0.5, None, ALU.mult)
        nc.scalar.activation(packed(zb[1][:]), woven(z[:, :, cols(1)]), ACT.Copy, scale=-0.5)
        for h in range(HALVES):
            nc.vector.quantize_mx(
                out=zq_w[h][:].bitcast(FP8X4), scales=zq_s[h][:], in_=zb[h][:].rearrange("p j t -> p (j t)")
            )
            for t in range(PACK):
                nc.tensor.matmul_mx(
                    out=s_ps[t][:, cols(h)],
                    lhsT=xc_w[:, P * t : P * (t + 1)].bitcast(FP8X4),
                    lhsT_scale=xc_s[:, P * t : P * (t + 1)],
                    rhs=zq_w[h][:].bitcast(FP8X4),
                    rhs_scale=zq_s[h][:],
                    start=True,
                    stop=True,
                )

        top = [sbt(f"top{t}", [P, 1], F32) for t in range(PACK)]
        bias = [sbt(f"bias{t}", [P, 1], F32) for t in range(PACK)]
        ea2 = [sbt(f"ea2_{t}", [P, S], F32) for t in range(PACK)]
        den2 = sbt("den2", [P, PACK, S], F32)
        s3 = [sbt(f"s3_{h}", [P, PACK, HALF], F32) for h in range(HALVES)]
        num = [sbt(f"num{h}", [P, PACK, HALF], F32) for h in range(HALVES)]
        inv = [sbt(f"inv{h}", [P, PACK, HALF], F32) for h in range(HALVES)]
        res = [sbt(f"res{h}", [P, PACK, HALF], F32) for h in range(HALVES)]
        rb = [sbt(f"rb{h}", [P, HALF, PACK], BF16) for h in range(HALVES)]
        rq_w = sbt("rq_w", [P, S], U32)
        rq_s = sbt("rq_s", [P, S], U8)

        for t in range(PACK):
            nc.vector.tensor_scalar(s[t][:, :S], s_ps[t][:], 0.0625, None, ALU.mult, ALU.max, accum_out=top[t][:])
            nc.vector.tensor_scalar(bias[t][:], top[t][:], tau2_c[:, t : t + 1], -1.0, ALU.mult, ALU.mult)
            nc.scalar.activation(s3[0][:, t, :], s[t][:].indirect(part(n3_l, 0)), ACT.Copy)
            nc.scalar.activation(
                ea2[t][:], s[t][:].indirect(n4_l[:]), ACT.Exp, bias=bias[t][:], scale=tau2_c[:, t : t + 1]
            )
        for t in range(PACK):
            nc.vector.tensor_tensor(num[0][:, t, :], s[t][:, cols(0)], s3[0][:, t, :], ALU.subtract)
            if t == PACK - 1:
                late = ea2[t][:, cols(1)]
                nc.vector.tensor_scalar(den2[:, t, cols(0)], ea2[t][:, cols(0)], 2.0, 0.5, ALU.mult, ALU.add)
                nc.vector.scalar_tensor_tensor(den2[:, t, cols(1)], late, 0.5, late, ALU.add, ALU.mult)
                nc.vector.reciprocal(inv[0][:, t, :], den2[:, t, cols(0)])
                nc.vector.tensor_tensor(res[0][:, t, :], num[0][:, t, :], inv[0][:, t, :], ALU.mult)
            else:
                nc.vector.scalar_tensor_tensor(den2[:, t, :], ea2[t][:], 0.5, ea2[t][:], ALU.add, ALU.mult)

        out_rows = out_0.rearrange("(p t) j -> p t j", t=PACK)
        out_words = out_1[0].rearrange("p j r -> p (j r)").bitcast(I32)

        def finish(h, queue):
            queue.dma_start(out_rows[:, :, cols(h)], res[h][:])
            nc.vector.tensor_copy(packed(rb[h][:]), woven(res[h][:]))
            nc.vector.quantize_mx(
                out=rq_w[:, cols(h)].bitcast(FP8X4), scales=rq_s[:, cols(h)], in_=rb[h][:].rearrange("p j t -> p (j t)")
            )
            queue.dma_start(out_words[:, cols(h)], rq_w[:, cols(h)].bitcast(I32))

        for pair in (slice(0, 2), slice(2, 3)):
            nc.scalar.activation(inv[0][:, pair, :], den2[:, pair, cols(0)], ACT.Abs_reciprocal_sqrt, bias=0.25, scale=4.0)
            nc.vector.tensor_tensor(res[0][:, pair, :], num[0][:, pair, :], inv[0][:, pair, :], ALU.mult)
        finish(0, nc.sync)
        for t in range(PACK):
            nc.scalar.activation(s3[1][:, t, :], s[t][:].indirect(part(n3_l, 1)), ACT.Copy)
            nc.vector.tensor_tensor(num[1][:, t, :], s[t][:, cols(1)], s3[1][:, t, :], ALU.subtract)
        for t in range(PACK):
            nc.scalar.activation(inv[1][:, t, :], den2[:, t, cols(1)], ACT.Abs_reciprocal_sqrt, bias=0.25, scale=4.0)
            nc.vector.tensor_tensor(res[1][:, t, :], num[1][:, t, :], inv[1][:, t, :], ALU.mult)
        finish(1, nc.sync)
        for q in range(QUADS):
            queue = nc.sync if q == QUADS - 1 else nc.scalar
            queue.dma_start(out_2[0, 4 * q : 4 * q + 4, :].bitcast(I32), rq_s[32 * q : 32 * q + 4, :].bitcast(I32))
